import numpy as np
import ml_dtypes


def mxq(x, axis, fmt="e4m3"):
    dtype, down = {"e4m3": (ml_dtypes.float8_e4m3fn, 7), "e5m2": (ml_dtypes.float8_e5m2, 14)}[fmt]
    v = np.moveaxis(np.asarray(x, np.float32).astype(ml_dtypes.bfloat16).astype(np.float64), axis, -1)
    blocks = v.reshape(v.shape[:-1] + (-1, 32))
    amax = np.abs(blocks).max(-1, keepdims=True)
    byte = np.maximum(np.where(amax > 0, np.frexp(amax)[1] - 1 + 127, 0) - down, 1)
    scale = np.exp2(byte - 127.0)
    codes = (blocks / scale).astype(np.float32).astype(dtype).astype(np.float64)
    return np.moveaxis((codes * scale).reshape(v.shape), -1, axis)


WIDE = False


def mx_kscale(k):
    if not WIDE:
        return np.ones(k)
    levels = np.array([10, -10, 5, -5, 0])
    if k % 512:
        return np.exp2(np.random.permutation(np.resize(levels, k // 32))).repeat(32)
    a = np.empty((k // 512, 16))
    for p in range(k // 512):
        a[p, :8] = np.random.permutation(np.resize(levels, 8))
        for g in range(8):
            far = levels[np.abs(levels - a[p, g]) >= 10]
            a[p, g + 8] = far[np.random.randint(len(far))]
    return np.exp2(a.ravel()).repeat(32)


def f64(x):
    return np.asarray(x).astype(np.float64)


def striped(idx):
    return np.tile(idx.reshape(-1, 16).T, (8, 1)).astype(np.uint16)


def unstriped(offs):
    return offs[:16].T.reshape(-1).astype(np.int64)


E2M1 = np.array([0.0, 0.5, 1.0, 1.5, 2.0, 3.0, 4.0, 6.0, -0.0, -0.5, -1.0, -1.5, -2.0, -3.0, -4.0, -6.0])


def pack_weight(w, fmt):
    k, n = w.shape
    w = f64(np.asarray(w, np.float32).astype(ml_dtypes.bfloat16)).reshape(k // 32, 32, n)
    amax = np.abs(w).max(1)
    if fmt == "e4m3":
        byte = np.frexp(amax)[1] - 1 + 127 - 7
    else:
        mant, ex = np.frexp(amax / 6.0)
        byte = np.where(mant > 0.5, ex, ex - 1) + 127
    byte = np.clip(np.where(amax > 0, byte, 1), 1, 254)
    scaled = (w * np.exp2(127.0 - byte)[:, None, :]).reshape(k, n).astype(np.float32)
    by_word = np.ascontiguousarray(scaled.reshape(k // 512, 128, 4, n).transpose(0, 1, 3, 2))
    if fmt == "e4m3":
        words = by_word.astype(ml_dtypes.float8_e4m3fn).view(np.uint8)
    else:
        c = by_word.astype(ml_dtypes.float4_e2m1fn).view(np.uint8) & 0xF
        words = (c[..., 0::2] | (c[..., 1::2] << 4)).reshape(k // 512, 128, 2 * n)
    return np.ascontiguousarray(words), np.ascontiguousarray(byte.astype(np.uint8).reshape(k // 512, 16, n))


def unpack_weight(words, scales, fmt):
    g, _, n = scales.shape
    words = np.ascontiguousarray(words).reshape(g, 128, n, -1)
    if fmt == "e4m3":
        vals = words.view(ml_dtypes.float8_e4m3fn).astype(np.float64)
    else:
        nib = np.empty((g, 128, n, 4), np.uint8)
        nib[..., 0::2] = words & 0xF
        nib[..., 1::2] = words >> 4
        vals = E2M1[nib]
    vals = vals * np.repeat(np.exp2(scales.astype(np.float64) - 127.0), 8, axis=1)[..., None]
    return vals.transpose(0, 1, 3, 2).reshape(g * 512, n)


def pack_table(v):
    words, scales = pack_weight(v, "e4m3")
    return np.concatenate([words.reshape(words.shape[0], -1), scales.reshape(scales.shape[0], -1)], axis=1)


def unpack_table(tab):
    g, t = tab.shape[0], tab.shape[1] // 528
    return unpack_weight(tab[:, :512 * t].reshape(g, 128, t, 4), tab[:, 512 * t:].reshape(g, 16, t), "e4m3")


K, R, M, T, S = 1024, 512, 1024, 2048, 512


def setup_inputs():
    n = np.random.standard_normal
    s = mx_kscale(K)[:, None]
    u = mx_kscale(R)[:, None]
    p_w4 = pack_weight(n((K, M)) / np.sqrt(K) / s, "e2m1")
    return {
        "tab": pack_table(n((K, T)) * s),
        "w4_words": p_w4[0],
        "w4_scales": p_w4[1],
        "down": (n((K, R)) / np.sqrt(K) / s * u.T).astype(np.float32),
        "up": (0.5 * n((R, M)) / np.sqrt(R) / u).astype(np.float32),
        "offs": striped(np.random.permutation(T)[:S]),
    }


def reference(tab, w4_words, w4_scales, down, up, offs):
    tab_ = unpack_table(tab)[:, unstriped(offs)]
    w4_ = unpack_weight(w4_words, w4_scales, "e2m1")
    down_ = mxq(f64(down), 0, "e4m3")
    up_ = mxq(f64(up), 0, "e4m3")
    h_ = mxq(down_.T @ tab_, 0, "e4m3")
    y = w4_.T @ tab_ + up_.T @ h_
    return y

from contextlib import ExitStack

import concourse.mybir as mybir

K, R, M, T, S = 1024, 512, 1024, 2048, 512

FLOPS = 2 * S * (K * R + K * M + R * M)

F32 = mybir.dt.float32
BF16 = mybir.dt.bfloat16
I32 = mybir.dt.int32
U32 = mybir.dt.uint32
U16 = mybir.dt.uint16
U8 = mybir.dt.uint8
E4M3 = mybir.dt.float8_e4m3fn_x4
E2M1 = mybir.dt.float4_e2m1fn_x4

P = 128
PACK = 4
PASSES = K // (P * PACK)
N_TILES = M // P
HELD = 5
CHUNK = 128
UP_HALF = M // 2


def tile_list_tablora_none_kernel(tc, tab, w4_words, w4_scales, down, up, offs, out):
    nc = tc.nc
    with ExitStack() as ctx:
        pool = ctx.enter_context(tc.tile_pool(name="keep", bufs=1))
        held = ctx.enter_context(tc.psum_pool(name="held", bufs=1))
        ring = ctx.enter_context(tc.psum_pool(name="ring", bufs=N_TILES - HELD))

        offsets = pool.tile([P, S // 16], U16, name="offsets")
        words = pool.tile([P, PASSES, T], I32, name="words", align_bytes=64)
        tscales = pool.tile([P, PASSES, T // 4], I32, name="tscales", align_bytes=64)
        w4w = pool.tile([P, PASSES, M // 2], I32, name="w4w", align_bytes=64)
        w4s = pool.tile([P, PASSES, M // 4], I32, name="w4s", align_bytes=64)
        raw0 = pool.tile([P, PACK * R], F32, name="raw0", align_bytes=64)
        raw = pool.tile([P, 3, PACK * R], F32, name="raw", align_bytes=64)
        down_raw = [raw0[:], raw[:, 0, :]]
        up_raw = [raw[:, 1, :], raw[:, 2, :]]

        nc.sync.dma_start(offsets[:], offs)

        def load_down(a):
            nc.sync.dma_start(
                out=down_raw[a], in_=down[512 * a : 512 * (a + 1), :].rearrange("(p j) r -> p (j r)", j=PACK)
            )

        def load_words(a):
            nc.sync.dma_start(
                out=words[:, a, :], in_=tab[a, 0 : 512 * T].rearrange("(p b) -> p b", p=P).bitcast(I32)
            )

        def load_w4(a):
            nc.sync.dma_start(out=w4w[:, a, :], in_=w4_words[a].bitcast(I32))

        def load_up(h):
            nc.sync.dma_start(
                out=up_raw[h].rearrange("p (j n) -> p j n", j=PACK),
                in_=up.rearrange("(p j) n -> p j n", j=PACK)[:, :, UP_HALF * h : UP_HALF * (h + 1)],
            )

        load_down(0)
        nc.vector.memset(tscales[:], 0)
        nc.gpsimd.memset(w4s[:], 0)
        nc.vector.memset(words[:, :, 0:1], 0)
        nc.vector.memset(raw[:, :, 0:1], 0.0)
        nc.vector.memset(w4w[:, :, 0:1], 0)

        tab_scale_rows = tab[:, 512 * T : 528 * T].rearrange("a (g r t) -> r g a t", g=4, r=4)
        w4_scale_rows = w4_scales.rearrange("a (g r) n -> r g a n", r=4)
        for r in range(4):
            nc.sync.dma_start(out=tscales[r:P:32, :, :], in_=tab_scale_rows[r].bitcast(I32))
        load_words(0)
        for r in range(4):
            nc.sync.dma_start(out=w4s[r:P:32, :, :], in_=w4_scale_rows[r].bitcast(I32))
        load_down(1)
        load_w4(0)
        load_words(1)
        load_w4(1)
        load_up(0)
        load_up(1)

        down_bf = [pool.tile([P, PACK * R], BF16, name=f"down_bf{a}", align_bytes=64) for a in range(PASSES)]
        down_c = [pool.tile([P, R], U32, name=f"down_c{a}", align_bytes=64) for a in range(PASSES)]
        down_s = [pool.tile([P, R], U8, name=f"down_s{a}", align_bytes=64) for a in range(PASSES)]

        def cast_down(copy, a, m0, m1):
            src = down_raw[a].rearrange("p (j m t) -> p m j t", j=PACK, t=PACK)
            dst = down_bf[a][:].rearrange("p (t m j) -> p m j t", t=PACK, j=PACK)
            copy(out=dst[:, m0:m1], in_=src[:, m0:m1])

        def quant_down(a):
            nc.vector.quantize_mx(out=down_c[a][:].bitcast(E4M3), scales=down_s[a][:], in_=down_bf[a][:])

        gw = [pool.tile([P, S], U32, name=f"gw{a}", align_bytes=64) for a in range(PASSES)]
        gs = [pool.tile([P, S], U8, name=f"gs{a}", align_bytes=64) for a in range(PASSES)]

        def gather_scales(a):
            nc.vector.tensor_copy(gs[a][:], tscales[:, a, :].bitcast(U8).indirect(offsets[:]))

        def gather_words(a, j0, j1):
            nc.vector.tensor_copy(
                gw[a][:, j0:j1], words[:, a, :].bitcast(U32).indirect(offsets[:, j0 // 16 : j1 // 16])
            )

        cast_down(nc.scalar.copy, 0, 0, 128)
        gather_scales(0)
        gather_words(0, 0, S)
        gather_scales(1)
        quant_down(0)

        w4_words_u8 = w4w[:].bitcast(U8)
        w4_scales_u8 = w4s[:].bitcast(U8)

        def base(acc, i, a):
            nc.tensor.matmul_mx(
                out=acc,
                lhsT=w4_words_u8[:, a, 2 * P * i : 2 * P * (i + 1)].bitcast(E2M1),
                lhsT_scale=w4_scales_u8[:, a, P * i : P * (i + 1)],
                rhs=gw[a][:].bitcast(E4M3),
                rhs_scale=gs[a][:],
                start=(a == 0),
                stop=False,
            )

        acc = [held.tile([P, S], F32, name=f"acc{i}") for i in range(HELD)]
        for i in range(HELD):
            base(acc[i][:], i, 0)

        cast_down(nc.vector.tensor_copy, 1, 0, 80)
        cast_down(nc.scalar.copy, 1, 80, 128)
        quant_down(1)
        gather_words(1, 0, S // 2)
        gather_words(1, S // 2, S)

        h_bf = pool.tile([P, PACK * S], BF16, name="h_bf", align_bytes=64)
        h_c = pool.tile([P, S], U32, name="h_c", align_bytes=64)
        h_s = pool.tile([P, S], U8, name="h_s", align_bytes=64)
        for c in range(S // CHUNK):
            cols = slice(CHUNK * c, CHUNK * (c + 1))
            bank = ring.tile([P, S], F32, name="bank")
            planes = bank[:].rearrange("p (t s) -> p t s", t=PACK)
            for t in range(PACK):
                for a in range(PASSES):
                    nc.tensor.matmul_mx(
                        out=planes[:, t, :],
                        lhsT=down_c[a][:, P * t : P * (t + 1)].bitcast(E4M3),
                        lhsT_scale=down_s[a][:, P * t : P * (t + 1)],
                        rhs=gw[a][:, cols].bitcast(E4M3),
                        rhs_scale=gs[a][:, cols],
                        start=(a == 0),
                        stop=(a == PASSES - 1),
                    )
            h_cols = h_bf[:, PACK * CHUNK * c : PACK * CHUNK * (c + 1)]
            nc.scalar.copy(
                out=h_cols.rearrange("p (s t) -> p s t", t=PACK), in_=planes.rearrange("p t s -> p s t")
            )
            nc.vector.quantize_mx(out=h_c[:, cols].bitcast(E4M3), scales=h_s[:, cols], in_=h_cols)

        up_bf = pool.tile([P, PACK * M], BF16, name="up_bf", align_bytes=64)
        up_c = pool.tile([P, M], U32, name="up_c", align_bytes=64)
        up_s = pool.tile([P, M], U8, name="up_s", align_bytes=64)

        def cast_up(copy, i):
            half, col = divmod(P * i, UP_HALF)
            src = up_raw[half].rearrange("p (j n) -> p j n", j=PACK)[:, :, col : col + P]
            dst = up_bf[:, PACK * P * i : PACK * P * (i + 1)]
            copy(
                out=dst.rearrange("p (c i j) -> p c j i", i=4, j=PACK),
                in_=src.rearrange("p j (c i) -> p c j i", i=4),
            )

        def quant_up(i):
            cols = slice(P * i, P * (i + 1))
            nc.vector.quantize_mx(
                out=up_c[:, cols].bitcast(E4M3), scales=up_s[:, cols], in_=up_bf[:, PACK * P * i : PACK * P * (i + 1)]
            )

        scalar_casts = (2, 6)
        vector_outs = (1, 4, 6)
        for i in range(N_TILES):
            cast_up(nc.scalar.copy if i in scalar_casts else nc.vector.tensor_copy, i)
            quant_up(i)

        for i in range(N_TILES):
            if i < HELD:
                bank = acc[i]
            else:
                bank = ring.tile([P, S], F32, name="bank")
                base(bank[:], i, 0)
            base(bank[:], i, 1)
            cols = slice(P * i, P * (i + 1))
            nc.tensor.matmul_mx(
                out=bank[:],
                lhsT=up_c[:, cols].bitcast(E4M3),
                lhsT_scale=up_s[:, cols],
                rhs=h_c[:].bitcast(E4M3),
                rhs_scale=h_s[:],
                start=False,
                stop=True,
            )
            staged = pool.tile([P, S], F32, name=f"staged{i}")
            (nc.vector.tensor_copy if i in vector_outs else nc.scalar.copy)(out=staged[:], in_=bank[:])
            nc.sync.dma_start(out=out[cols, :], in_=staged[:])
